import numpy as np
import ml_dtypes


def mxq(x, axis, fmt="e4m3"):
    dtype, down = {"e4m3": (ml_dtypes.float8_e4m3fn, 7), "e5m2": (ml_dtypes.float8_e5m2, 14)}[fmt]
    v = np.moveaxis(np.asarray(x, np.float32).astype(ml_dtypes.bfloat16).astype(np.float64), axis, -1)
    blocks = v.reshape(v.shape[:-1] + (-1, 32))
    amax = np.abs(blocks).max(-1, keepdims=True)
    byte = np.maximum(np.where(amax > 0, np.frexp(amax)[1] - 1 + 127, 0) - down, 1)
    scale = np.exp2(byte - 127.0)
    codes = (blocks / scale).astype(np.float32).astype(dtype).astype(np.float64)
    return np.moveaxis((codes * scale).reshape(v.shape), -1, axis)


WIDE = False


def mx_kscale(k):
    if not WIDE:
        return np.ones(k)
    levels = np.array([10, -10, 5, -5, 0])
    if k % 512:
        return np.exp2(np.random.permutation(np.resize(levels, k // 32))).repeat(32)
    a = np.empty((k // 512, 16))
    for p in range(k // 512):
        a[p, :8] = np.random.permutation(np.resize(levels, 8))
        for g in range(8):
            far = levels[np.abs(levels - a[p, g]) >= 10]
            a[p, g + 8] = far[np.random.randint(len(far))]
    return np.exp2(a.ravel()).repeat(32)


def f64(x):
    return np.asarray(x).astype(np.float64)


def striped(idx):
    return np.tile(idx.reshape(-1, 16).T, (8, 1)).astype(np.uint16)


def unstriped(offs):
    return offs[:16].T.reshape(-1).astype(np.int64)


def striped8(idx):
    return np.concatenate([x.reshape(-1, 16).T for x in idx]).astype(np.uint16)


def runs(offs, k):
    lists = np.stack([offs[16 * r : 16 * r + 16].T.reshape(-1) for r in range(8)]).astype(np.int64)
    return lists[np.arange(k) % 512 // 64]


def pack_weight(w):
    k, n = w.shape
    w = f64(np.asarray(w, np.float32).astype(ml_dtypes.bfloat16)).reshape(k // 32, 32, n)
    amax = np.abs(w).max(1)
    byte = np.clip(np.where(amax > 0, np.frexp(amax)[1] - 1 + 127 - 7, 1), 1, 254)
    scaled = (w * np.exp2(127.0 - byte)[:, None, :]).reshape(k, n).astype(np.float32)
    words = np.ascontiguousarray(scaled.reshape(k // 512, 128, 4, n).transpose(0, 1, 3, 2)).astype(ml_dtypes.float8_e4m3fn).view(np.uint8)
    return words, np.ascontiguousarray(byte.astype(np.uint8).reshape(k // 512, 16, n))


def unpack_weight(words, scales):
    g, p, n, _ = words.shape
    vals = np.ascontiguousarray(words).view(ml_dtypes.float8_e4m3fn).astype(np.float64) * np.repeat(np.exp2(scales.astype(np.float64) - 127.0), 8, axis=1)[..., None]
    return vals.transpose(0, 1, 3, 2).reshape(g * 512, n)


def sigmoid(v):
    return 1.0 / (1.0 + np.exp(-np.maximum(v, -700.0)))

def planes(y):
    n, m = y.shape
    v = y.astype(np.float32).astype(ml_dtypes.bfloat16).astype(np.float64).reshape(n // 32, 32, m)
    top = np.abs(v).max(1)
    byte = np.clip(np.where(top > 0, np.frexp(top)[1] - 1 + 127 - 7, 1), 1, 254)
    codes = (v * np.exp2(127.0 - byte)[:, None, :]).reshape(n, m).astype(np.float32).astype(ml_dtypes.float8_e4m3fn).view(np.uint8)
    words = codes.reshape(n // 512, 128, 4, m).transpose(0, 1, 3, 2)
    return np.ascontiguousarray(words), np.ascontiguousarray(byte.astype(np.uint8).reshape(n // 512, 16, m))


K, T, S, G, H = 512, 1024, 512, 2048, 512


def setup_inputs():
    n = np.random.standard_normal
    s = mx_kscale(K)[:, None]
    packed_xT = pack_weight(n((K, T)) * s)
    packed_dT = pack_weight(n((K, G)) / s)
    return {
        "x_words": packed_xT[0],
        "x_scales": packed_xT[1],
        "d_words": packed_dT[0],
        "d_scales": packed_dT[1],
        "gs": (np.random.uniform(0.5, 1.5, (K, 1)) * s).astype(np.float32),
        "sl": np.random.uniform(1.5, 3.0, (H, 1)).astype(np.float32),
        "th": (0.5 * n((H, 1))).astype(np.float32),
        "offs": striped(np.random.permutation(T)[:S]),
        "k1": striped8(np.random.randint(0, G, (8, H))),
        "n1": striped(np.random.permutation(S)),
        "n2": striped(np.random.permutation(S)),
        "k2": striped8(np.random.randint(0, G, (8, H))),
        "n3": striped8(np.stack([np.random.permutation(S) for _ in range(8)])),
        "n4": striped8(np.stack([np.random.permutation(S) for _ in range(8)])),
    }


def reference(x_words, x_scales, d_words, d_scales, gs, sl, th, offs, k1, n1, n2, k2, n3, n4):
    d_k2 = unpack_weight(d_words, d_scales)[np.arange(K)[:, None], runs(k2, K)]
    d_k1 = unpack_weight(d_words, d_scales)[np.arange(K)[:, None], runs(k1, K)]
    xq = unpack_weight(x_words, x_scales)[:, unstriped(offs)]
    h = 0.0625 * (d_k1.T @ xq)
    sm = np.maximum(h, h[:, unstriped(n2)])
    ds = np.zeros((H, S))
    ds[:, unstriped(n1)] = sm
    z = f64(gs) * (ds * sigmoid(h))
    h2 = 0.0625 * ((d_k2.T @ mxq(z, 0, "e4m3")))
    sg = sigmoid(f64(sl) * (h2[np.arange(H)[:, None], runs(n3, H)] - f64(th)))
    out_0 = 1.5 * (h2 * (sg - (sg[np.arange(H)[:, None], runs(n4, H)])))
    return (out_0,) + planes(out_0)

@@ -1,0 +1,269 @@
+from contextlib import ExitStack
+
+import concourse.mybir as mybir
+
+K, T, S, G, H = 512, 1024, 512, 2048, 512
+FLOPS = 2 * 2 * K * H * S
+
+F32 = mybir.dt.float32
+BF16 = mybir.dt.bfloat16
+I32 = mybir.dt.int32
+U32 = mybir.dt.uint32
+U16 = mybir.dt.uint16
+U8 = mybir.dt.uint8
+FP8X4 = mybir.dt.float8_e4m3fn_x4
+MULT = mybir.AluOpType.mult
+MAX = mybir.AluOpType.max
+ADD = mybir.AluOpType.add
+SUB = mybir.AluOpType.subtract
+COPY = mybir.ActivationFunctionType.Copy
+SIGMOID = mybir.ActivationFunctionType.Sigmoid
+
+P = 128
+PACK = 4
+HALF = S // 2
+LCOLS = S // 16
+LHALF = LCOLS // 2
+H_SPARE = 16
+DS_WIDE = 704
+
+
+def tile_picked_codesendgedb_none_po_kernel(
+    tc, x_words, x_scales, d_words, d_scales, gs, sl, th, offs, k1, n1, n2, k2, n3, n4, out_0, out_1, out_2
+):
+    nc = tc.nc
+    with ExitStack() as ctx:
+        lists = ctx.enter_context(tc.tile_pool(name="lists", bufs=1))
+        keep = ctx.enter_context(tc.tile_pool(name="keep", bufs=1))
+        psum = ctx.enter_context(tc.psum_pool(name="psum", bufs=1))
+
+        def load_list(src, name):
+            tile = lists.tile([P, LCOLS], U16, name=name)
+            nc.sync.dma_start(tile[:], src)
+            return tile
+
+        def sb(shape, dtype, name, tag=None):
+            return keep.tile(shape, dtype, name=name, tag=tag or name, align_bytes=64)
+
+        def words_view(dram):
+            return dram[0].rearrange("p n t -> p (n t)").bitcast(I32)
+
+        d_byte_win = sb([P, G], U8, "d_byte_win")
+        x_byte_win = sb([P, T], U8, "x_byte_win")
+        d_word_win = sb([P, G], U32, "d_word_win")
+        x_word_win = sb([P, T], U32, "x_word_win")
+
+        def rows_view(dram, width):
+            return dram[0].bitcast(I32).unsqueeze(1).to_broadcast([16, 8, width // 4])
+
+        offs_t = load_list(offs, "offs_t")
+        nc.sync.dma_start(x_byte_win[:].bitcast(I32), rows_view(x_scales, T))
+        k1_t = load_list(k1, "k1_t")
+        nc.sync.dma_start(d_byte_win[:].bitcast(I32), rows_view(d_scales, G))
+        nc.sync.dma_start(d_word_win[:].bitcast(I32), words_view(d_words))
+        n2_t = load_list(n2, "n2_t")
+        n1_t = load_list(n1, "n1_t")
+        nc.sync.dma_start(x_word_win[:].bitcast(I32), words_view(x_words))
+        n3_t = load_list(n3, "n3_t")
+        n4_t = load_list(n4, "n4_t")
+        k2_t = load_list(k2, "k2_t")
+
+        placed1 = sb([P, H + S], U8, "placed1")
+        w2_bytes = sb([P, H], U8, "w2_bytes")
+        nc.vector.memset(placed1[:].bitcast(I32), 0)
+        nc.vector.memset(w2_bytes[:].bitcast(I32), 0)
+        h_win = [sb([P, S + H_SPARE], F32, "h_win%d" % t) for t in range(PACK)]
+        for t in range(PACK):
+            nc.vector.memset(h_win[t][:, S:], 0.0)
+
+        def load_rows(src, name):
+            tile = sb([P, PACK], F32, name)
+            nc.gpsimd.dma_start(tile[:], src.rearrange("(p t) o -> p (t o)", t=PACK))
+            return tile
+
+        gs_t = load_rows(gs, "gs_t")
+        sl_t = load_rows(sl, "sl_t")
+        th_t = load_rows(th, "th_t")
+
+        def deal_bytes(dealt, picked):
+            nc.vector.tensor_copy(
+                dealt.rearrange("p (t m) -> p t m", t=PACK), picked.rearrange("p (m t) -> p t m", t=PACK)
+            )
+
+        def place_bytes(placed, dealt, queues):
+            for r in range(4):
+                queues[r % len(queues)].dma_start(placed[r:P:32, :].bitcast(I32), dealt[8 * r : P : 32, :].bitcast(I32))
+
+        def pick_words(lst, name, tag=None):
+            picked = sb([P, H], U32, name + "_picked", tag)
+            dealt = sb([P, H], U32, name + "_dealt")
+            nc.vector.tensor_copy(picked[:], d_word_win[:].indirect(lst[:]))
+            nc.vector.tensor_copy(
+                dealt[:].rearrange("p (t m i) -> p m t i", t=PACK, i=4),
+                picked[:].rearrange("p (m i t) -> p m t i", t=PACK, i=4),
+            )
+            return dealt
+
+        w1_picked = sb([P, H], U8, "w1_picked")
+        xq_picked = sb([P, S], U8, "xq_picked")
+        dealt1 = sb([P, H + S], U8, "dealt1")
+        nc.vector.tensor_copy(xq_picked[:], x_byte_win[:].indirect(offs_t[:]))
+        nc.vector.tensor_copy(w1_picked[:], d_byte_win[:].indirect(k1_t[:]))
+        nc.vector.tensor_copy(dealt1[:, H:].bitcast(I32), xq_picked[:].bitcast(I32))
+        deal_bytes(dealt1[:, :H], w1_picked[:])
+        place_bytes(placed1, dealt1, [nc.sync])
+        w1_bytes = placed1[:, :H]
+        xq_bytes = placed1[:, H:]
+        w1_words = pick_words(k1_t, "w1_words", "w1_picked")
+        xq_words = sb([P, S], U32, "xq_words", "w1_picked")
+        nc.vector.tensor_copy(xq_words[:], x_word_win[:].indirect(offs_t[:]))
+
+        acc1 = [psum.tile([P, S], F32, name="acc1_%d" % t, tag="bank%d" % t) for t in range(PACK)]
+        for t in range(PACK):
+            cols = slice(P * t, P * (t + 1))
+            nc.tensor.matmul_mx(
+                out=acc1[t][:],
+                lhsT=w1_words[:, cols].bitcast(FP8X4),
+                lhsT_scale=w1_bytes[:, cols],
+                rhs=xq_words[:].bitcast(FP8X4),
+                rhs_scale=xq_bytes,
+                start=True,
+                stop=True,
+            )
+
+        w2_picked = sb([P, H], U8, "w2_picked", "x_word_win")
+        dealt2 = sb([P, H], U8, "dealt2")
+        nc.vector.tensor_copy(w2_picked[:], d_byte_win[:].indirect(k2_t[:]))
+        deal_bytes(dealt2[:], w2_picked[:])
+        place_bytes(w2_bytes, dealt2, [nc.sync])
+        w2_words = pick_words(k2_t, "w2_words", "x_word_win")
+        bias = sb([P, PACK], F32, "bias")
+        sl_th = sb([P, PACK], F32, "sl_th")
+        nc.gpsimd.tensor_tensor(sl_th[:], sl_t[:], th_t[:], MULT)
+        nc.gpsimd.tensor_scalar(bias[:], sl_th[:], -1.0, 0.0, MULT, ADD)
+
+        h2_win = [sb([P, 2 * S], F32, "h2_win%d" % t) for t in range(PACK)]
+        sg_win = [sb([P, 2 * S], F32, "sg_win%d" % t) for t in range(PACK)]
+        fetched = [sg_win[t][:, S:] for t in range(PACK)]
+        sm = [sb([P, S], F32, "sm%d" % t) for t in range(PACK)]
+        ds = [sb([P, DS_WIDE if t in (0, 3) else S], F32, "ds%d" % t) for t in range(PACK)]
+        z = sb([P, PACK, S], F32, "z")
+
+        for t in range(PACK):
+            if t == 0:
+                nc.scalar.activation(h2_win[0][:, S:], acc1[0][:], SIGMOID, scale=0.0625)
+            nc.scalar.activation(h_win[t][:, :S], acc1[t][:], COPY, scale=0.0625)
+            nc.scalar.activation(fetched[t], h_win[t][:].indirect(n2_t[:]), COPY)
+            nc.vector.scalar_tensor_tensor(sm[t][:], acc1[t][:], 0.0625, fetched[t], MULT, MAX)
+            if t in (0, 3):
+                nc.vector.tensor_copy(ds[t][:].indirect(n1_t[:]), sm[t][:])
+        for t in range(1, PACK):
+            nc.scalar.activation(h2_win[t][:, S:], h_win[t][:, :S], SIGMOID)
+
+        nc.scalar.activation(ds[1][:].indirect(n1_t[:, :24]), sm[1][:, :384], COPY)
+        nc.vector.tensor_copy(ds[1][:].indirect(n1_t[:, 24:]), sm[1][:, 384:])
+        nc.scalar.activation(ds[2][:].indirect(n1_t[:, :LHALF]), sm[2][:, :HALF], COPY)
+        nc.scalar.activation(ds[2][:].indirect(n1_t[:, LHALF:]), sm[2][:, HALF:], COPY)
+
+        halves = [slice(0, HALF), slice(HALF, S)]
+        for t in (0, 3, 1):
+            nc.vector.scalar_tensor_tensor(
+                z[:, t, :], ds[t][:, :S], gs_t[:, t : t + 1], h2_win[t][:, S:], MULT, MULT
+            )
+        for a in range(2):
+            nc.vector.scalar_tensor_tensor(
+                z[:, 2, halves[a]],
+                ds[2][:, halves[a]],
+                gs_t[:, 2:3],
+                h2_win[2][:, S + HALF * a : S + HALF * (a + 1)],
+                MULT,
+                MULT,
+            )
+
+        def interleave(eng_copy, dst, src):
+            eng_copy(
+                dst[:].rearrange("p (c i t) -> p c t i", i=4, t=PACK),
+                src.rearrange("p t (c i) -> p c t i", i=4),
+            )
+
+        zb = [sb([P, PACK * HALF], BF16, "zb%d" % a) for a in range(2)]
+        z_words = [sb([P, HALF], U32, "z_words%d" % a) for a in range(2)]
+        z_bytes = [sb([P, HALF], U8, "z_bytes%d" % a) for a in range(2)]
+        for a in range(2):
+            interleave(nc.vector.tensor_copy, zb[a], z[:, :, halves[a]])
+        for a in range(2):
+            nc.vector.quantize_mx(out=z_words[a][:].bitcast(FP8X4), scales=z_bytes[a][:], in_=zb[a][:])
+
+        acc2 = [
+            [psum.tile([P, HALF], F32, name="acc2_%d_%d" % (a, t), tag="bank%d" % (PACK * (1 - a) + t)) for t in range(PACK)]
+            for a in range(2)
+        ]
+        for t in range(PACK):
+            cols = slice(P * t, P * (t + 1))
+            for a in range(2):
+                nc.tensor.matmul_mx(
+                    out=acc2[a][t][:],
+                    lhsT=w2_words[:, cols].bitcast(FP8X4),
+                    lhsT_scale=w2_bytes[:, cols],
+                    rhs=z_words[a][:].bitcast(FP8X4),
+                    rhs_scale=z_bytes[a][:],
+                    start=True,
+                    stop=True,
+                )
+        for a in range(2):
+            nc.scalar.activation(h2_win[0][:, halves[a]], acc2[a][0][:], COPY, scale=0.0625)
+        for t in range(1, PACK):
+            for a in range(2):
+                nc.vector.tensor_scalar(h2_win[t][:, halves[a]], acc2[a][t][:], 0.0625, None, MULT)
+
+        far = [sb([P, S], F32, "far%d" % t) for t in range(PACK)]
+        diff = [sb([P, S], F32, "diff%d" % t) for t in range(PACK)]
+        y = sb([P, PACK, S], F32, "y")
+        yb = [sb([P, PACK * HALF], BF16, "yb%d" % a) for a in range(2)]
+        y_words = sb([P, S], U32, "y_words")
+        y_bytes = sb([P, S], U8, "y_bytes")
+        n4_halves = [n4_t[:, :LHALF], n4_t[:, LHALF:]]
+        out_rows = out_0.rearrange("(p t) c -> p t c", t=PACK)
+        out_words = out_1[0].rearrange("p n t -> p (n t)").bitcast(I32)
+
+        def subtract(t, cols):
+            nc.vector.tensor_tensor(diff[t][:, cols], sg_win[t][:, cols], far[t][:, cols], SUB)
+
+        def scale_out(t, cols):
+            nc.vector.scalar_tensor_tensor(y[:, t, cols], h2_win[t][:, cols], 1.5, diff[t][:, cols], MULT, MULT)
+            nc.sync.dma_start(out_rows[:, t, cols], y[:, t, cols])
+
+        whole = slice(0, S)
+        for t in range(PACK):
+            nc.scalar.activation(
+                sg_win[t][:, :S],
+                h2_win[t][:].indirect(n3_t[:]),
+                SIGMOID,
+                bias=bias[:, t : t + 1],
+                scale=sl_t[:, t : t + 1],
+            )
+        for t in range(2):
+            nc.vector.tensor_copy(far[t][:], sg_win[t][:].indirect(n4_t[:]))
+        nc.scalar.activation(far[2][:], sg_win[2][:].indirect(n4_t[:]), COPY)
+        for a in range(2):
+            nc.scalar.activation(far[3][:, halves[a]], sg_win[3][:].indirect(n4_halves[a]), COPY)
+        subtract(0, whole)
+        subtract(1, whole)
+        scale_out(0, whole)
+        scale_out(1, whole)
+        subtract(2, whole)
+        subtract(3, halves[0])
+        scale_out(2, whole)
+        subtract(3, halves[1])
+        scale_out(3, halves[0])
+        scale_out(3, halves[1])
+        interleave(nc.scalar.copy, yb[0], y[:, :, halves[0]])
+        interleave(nc.vector.tensor_copy, yb[1], y[:, :, halves[1]])
+        for a in (1, 0):
+            nc.vector.quantize_mx(out=y_words[:, halves[a]].bitcast(FP8X4), scales=y_bytes[:, halves[a]], in_=yb[a][:])
+            nc.sync.dma_start(out_words[:, halves[a]], y_words[:, halves[a]].bitcast(I32))
+        for q in range(4):
+            queue = nc.scalar if q % 2 == 0 else nc.sync
+            queue.dma_start(
+                out_2[0, 4 * q : 4 * q + 4, :].bitcast(I32), y_bytes[32 * q : 32 * q + 4, :].bitcast(I32)
+            )

@@ -35,6 +35,7 @@ def tile_picked_codesendgedb_none_po_kernel(
     with ExitStack() as ctx:
         lists = ctx.enter_context(tc.tile_pool(name="lists", bufs=1))
         keep = ctx.enter_context(tc.tile_pool(name="keep", bufs=1))
+        shared = ctx.enter_context(tc.tile_pool(name="shared", bufs=1))
         psum = ctx.enter_context(tc.psum_pool(name="psum", bufs=1))
 
         def load_list(src, name):
@@ -51,7 +52,7 @@ def tile_picked_codesendgedb_none_po_kernel(
         d_byte_win = sb([P, G], U8, "d_byte_win")
         x_byte_win = sb([P, T], U8, "x_byte_win")
         d_word_win = sb([P, G], U32, "d_word_win")
-        x_word_win = sb([P, T], U32, "x_word_win")
+        x_word_win = shared.tile([P, T], U32, name="x_word_win", offset=0, align_bytes=64)
 
         def rows_view(dram, width):
             return dram[0].bitcast(I32).unsqueeze(1).to_broadcast([16, 8, width // 4])
@@ -63,8 +64,8 @@ def tile_picked_codesendgedb_none_po_kernel(
         nc.sync.dma_start(d_word_win[:].bitcast(I32), words_view(d_words))
         n2_t = load_list(n2, "n2_t")
         n1_t = load_list(n1, "n1_t")
-        nc.sync.dma_start(x_word_win[:].bitcast(I32), words_view(x_words))
         n3_t = load_list(n3, "n3_t")
+        nc.sync.dma_start(x_word_win[:].bitcast(I32), words_view(x_words))
         n4_t = load_list(n4, "n4_t")
         k2_t = load_list(k2, "k2_t")
 
@@ -94,16 +95,14 @@ def tile_picked_codesendgedb_none_po_kernel(
             for r in range(4):
                 queues[r % len(queues)].dma_start(placed[r:P:32, :].bitcast(I32), dealt[8 * r : P : 32, :].bitcast(I32))
 
-        def pick_words(lst, name, tag=None):
-            picked = sb([P, H], U32, name + "_picked", tag)
-            dealt = sb([P, H], U32, name + "_dealt")
-            nc.vector.tensor_copy(picked[:], d_word_win[:].indirect(lst[:]))
+        def deal_words(dealt, picked):
             nc.vector.tensor_copy(
                 dealt[:].rearrange("p (t m i) -> p m t i", t=PACK, i=4),
                 picked[:].rearrange("p (m i t) -> p m t i", t=PACK, i=4),
             )
-            return dealt
 
+        halves = [slice(0, HALF), slice(HALF, S)]
+        whole = slice(0, S)
         w1_picked = sb([P, H], U8, "w1_picked")
         xq_picked = sb([P, S], U8, "xq_picked")
         dealt1 = sb([P, H + S], U8, "dealt1")
@@ -114,29 +113,42 @@ def tile_picked_codesendgedb_none_po_kernel(
         place_bytes(placed1, dealt1, [nc.sync])
         w1_bytes = placed1[:, :H]
         xq_bytes = placed1[:, H:]
-        w1_words = pick_words(k1_t, "w1_words", "w1_picked")
-        xq_words = sb([P, S], U32, "xq_words", "w1_picked")
-        nc.vector.tensor_copy(xq_words[:], x_word_win[:].indirect(offs_t[:]))
+        w1_words_picked = sb([P, H], U32, "w1_words_picked")
+        w1_words = sb([P, H], U32, "w1_words")
+        xq_words = sb([P, S], U32, "xq_words")
+        nc.vector.tensor_copy(w1_words_picked[:], d_word_win[:].indirect(k1_t[:]))
+        nc.vector.tensor_copy(xq_words[:, halves[0]], x_word_win[:].indirect(offs_t[:, :LHALF]))
+        deal_words(w1_words, w1_words_picked)
+        nc.vector.tensor_copy(xq_words[:, halves[1]], x_word_win[:].indirect(offs_t[:, LHALF:]))
 
-        acc1 = [psum.tile([P, S], F32, name="acc1_%d" % t, tag="bank%d" % t) for t in range(PACK)]
-        for t in range(PACK):
+        def product(out, w_words, w_bytes, t, r_words, r_bytes):
             cols = slice(P * t, P * (t + 1))
             nc.tensor.matmul_mx(
-                out=acc1[t][:],
-                lhsT=w1_words[:, cols].bitcast(FP8X4),
-                lhsT_scale=w1_bytes[:, cols],
-                rhs=xq_words[:].bitcast(FP8X4),
-                rhs_scale=xq_bytes,
+                out=out,
+                lhsT=w_words[:, cols].bitcast(FP8X4),
+                lhsT_scale=w_bytes[:, cols],
+                rhs=r_words.bitcast(FP8X4),
+                rhs_scale=r_bytes,
                 start=True,
                 stop=True,
             )
 
-        w2_picked = sb([P, H], U8, "w2_picked", "x_word_win")
+        first1 = [psum.tile([P, HALF], F32, name="first1_%d" % a, tag="bank%d" % a) for a in range(2)]
+        acc1 = [None] + [psum.tile([P, S], F32, name="acc1_%d" % t, tag="bank%d" % (t + 1)) for t in range(1, PACK)]
+        for a in range(2):
+            product(first1[a][:], w1_words, w1_bytes, 0, xq_words[:, halves[a]], xq_bytes[:, halves[a]])
+        for t in range(1, PACK):
+            product(acc1[t][:], w1_words, w1_bytes, t, xq_words[:], xq_bytes)
+
+        w2_picked = shared.tile([P, H], U8, name="w2_picked", offset=4 * H, align_bytes=64)
+        w2_words_picked = shared.tile([P, H], U32, name="w2_words_picked", offset=0, align_bytes=64)
         dealt2 = sb([P, H], U8, "dealt2")
+        w2_words = sb([P, H], U32, "w2_words")
         nc.vector.tensor_copy(w2_picked[:], d_byte_win[:].indirect(k2_t[:]))
+        nc.vector.tensor_copy(w2_words_picked[:], d_word_win[:].indirect(k2_t[:]))
         deal_bytes(dealt2[:], w2_picked[:])
         place_bytes(w2_bytes, dealt2, [nc.sync])
-        w2_words = pick_words(k2_t, "w2_words", "x_word_win")
+        deal_words(w2_words, w2_words_picked)
         bias = sb([P, PACK], F32, "bias")
         sl_th = sb([P, PACK], F32, "sl_th")
         nc.gpsimd.tensor_tensor(sl_th[:], sl_t[:], th_t[:], MULT)
@@ -151,25 +163,33 @@ def tile_picked_codesendgedb_none_po_kernel(
 
         for t in range(PACK):
             if t == 0:
-                nc.scalar.activation(h2_win[0][:, S:], acc1[0][:], SIGMOID, scale=0.0625)
-            nc.scalar.activation(h_win[t][:, :S], acc1[t][:], COPY, scale=0.0625)
+                nc.scalar.activation(h2_win[0][:, S : S + HALF], first1[0][:], SIGMOID, scale=0.0625)
+                for a in range(2):
+                    nc.scalar.activation(h_win[0][:, halves[a]], first1[a][:], COPY, scale=0.0625)
+                nc.scalar.activation(h2_win[0][:, S + HALF :], first1[1][:], SIGMOID, scale=0.0625)
+            else:
+                nc.scalar.activation(h_win[t][:, :S], acc1[t][:], COPY, scale=0.0625)
             nc.scalar.activation(fetched[t], h_win[t][:].indirect(n2_t[:]), COPY)
-            nc.vector.scalar_tensor_tensor(sm[t][:], acc1[t][:], 0.0625, fetched[t], MULT, MAX)
+            if t == 0:
+                nc.vector.tensor_tensor(sm[t][:], h_win[t][:, :S], fetched[t], MAX)
+            else:
+                nc.vector.scalar_tensor_tensor(sm[t][:], acc1[t][:], 0.0625, fetched[t], MULT, MAX)
             if t in (0, 3):
                 nc.vector.tensor_copy(ds[t][:].indirect(n1_t[:]), sm[t][:])
+            if t == 1:
+                nc.vector.tensor_copy(ds[1][:].indirect(n1_t[:, :14]), sm[1][:, :224])
         for t in range(1, PACK):
             nc.scalar.activation(h2_win[t][:, S:], h_win[t][:, :S], SIGMOID)
 
-        nc.scalar.activation(ds[1][:].indirect(n1_t[:, :24]), sm[1][:, :384], COPY)
-        nc.vector.tensor_copy(ds[1][:].indirect(n1_t[:, 24:]), sm[1][:, 384:])
+        nc.scalar.activation(ds[1][:].indirect(n1_t[:, 14:]), sm[1][:, 224:], COPY)
         nc.scalar.activation(ds[2][:].indirect(n1_t[:, :LHALF]), sm[2][:, :HALF], COPY)
         nc.scalar.activation(ds[2][:].indirect(n1_t[:, LHALF:]), sm[2][:, HALF:], COPY)
 
-        halves = [slice(0, HALF), slice(HALF, S)]
-        for t in (0, 3, 1):
-            nc.vector.scalar_tensor_tensor(
-                z[:, t, :], ds[t][:, :S], gs_t[:, t : t + 1], h2_win[t][:, S:], MULT, MULT
-            )
+        gated = [sb([P, S], F32, "gated%d" % t) for t in range(2)]
+        for t in range(2):
+            nc.gpsimd.tensor_scalar(gated[t][:], h2_win[t][:, S:], gs_t[:, t : t + 1], 0.0, MULT, ADD)
+            nc.gpsimd.tensor_tensor(z[:, t, :], ds[t][:, :S], gated[t][:], MULT)
+        nc.vector.scalar_tensor_tensor(z[:, 3, :], ds[3][:, :S], gs_t[:, 3:4], h2_win[3][:, S:], MULT, MULT)
         for a in range(2):
             nc.vector.scalar_tensor_tensor(
                 z[:, 2, halves[a]],
@@ -187,34 +207,23 @@ def tile_picked_codesendgedb_none_po_kernel(
             )
 
         zb = [sb([P, PACK * HALF], BF16, "zb%d" % a) for a in range(2)]
-        z_words = [sb([P, HALF], U32, "z_words%d" % a) for a in range(2)]
-        z_bytes = [sb([P, HALF], U8, "z_bytes%d" % a) for a in range(2)]
+        z_words = sb([P, S], U32, "z_words")
+        z_bytes = sb([P, S], U8, "z_bytes")
         for a in range(2):
             interleave(nc.vector.tensor_copy, zb[a], z[:, :, halves[a]])
         for a in range(2):
-            nc.vector.quantize_mx(out=z_words[a][:].bitcast(FP8X4), scales=z_bytes[a][:], in_=zb[a][:])
+            nc.vector.quantize_mx(out=z_words[:, halves[a]].bitcast(FP8X4), scales=z_bytes[:, halves[a]], in_=zb[a][:])
 
-        acc2 = [
-            [psum.tile([P, HALF], F32, name="acc2_%d_%d" % (a, t), tag="bank%d" % (PACK * (1 - a) + t)) for t in range(PACK)]
-            for a in range(2)
-        ]
-        for t in range(PACK):
-            cols = slice(P * t, P * (t + 1))
-            for a in range(2):
-                nc.tensor.matmul_mx(
-                    out=acc2[a][t][:],
-                    lhsT=w2_words[:, cols].bitcast(FP8X4),
-                    lhsT_scale=w2_bytes[:, cols],
-                    rhs=z_words[a][:].bitcast(FP8X4),
-                    rhs_scale=z_bytes[a][:],
-                    start=True,
-                    stop=True,
-                )
+        first2 = [psum.tile([P, HALF], F32, name="first2_%d" % a, tag="bank%d" % (5 + a)) for a in range(2)]
+        acc2 = [None] + [psum.tile([P, S], F32, name="acc2_%d" % t, tag="bank%d" % ((6 + t) % 8)) for t in range(1, PACK)]
         for a in range(2):
-            nc.scalar.activation(h2_win[0][:, halves[a]], acc2[a][0][:], COPY, scale=0.0625)
+            product(first2[a][:], w2_words, w2_bytes, 0, z_words[:, halves[a]], z_bytes[:, halves[a]])
         for t in range(1, PACK):
-            for a in range(2):
-                nc.vector.tensor_scalar(h2_win[t][:, halves[a]], acc2[a][t][:], 0.0625, None, MULT)
+            product(acc2[t][:], w2_words, w2_bytes, t, z_words[:], z_bytes[:])
+        for a in range(2):
+            nc.scalar.activation(h2_win[0][:, halves[a]], first2[a][:], COPY, scale=0.0625)
+        for t in range(1, PACK):
+            nc.vector.tensor_scalar(h2_win[t][:, :S], acc2[t][:], 0.0625, None, MULT)
 
         far = [sb([P, S], F32, "far%d" % t) for t in range(PACK)]
         diff = [sb([P, S], F32, "diff%d" % t) for t in range(PACK)]
@@ -226,14 +235,15 @@ def tile_picked_codesendgedb_none_po_kernel(
         out_rows = out_0.rearrange("(p t) c -> p t c", t=PACK)
         out_words = out_1[0].rearrange("p n t -> p (n t)").bitcast(I32)
 
-        def subtract(t, cols):
-            nc.vector.tensor_tensor(diff[t][:, cols], sg_win[t][:, cols], far[t][:, cols], SUB)
+        def subtract(engine, t, cols):
+            engine.tensor_tensor(diff[t][:, cols], sg_win[t][:, cols], far[t][:, cols], SUB)
 
-        def scale_out(t, cols):
-            nc.vector.scalar_tensor_tensor(y[:, t, cols], h2_win[t][:, cols], 1.5, diff[t][:, cols], MULT, MULT)
+        def scale_out(t, cols, acc):
+            nc.vector.scalar_tensor_tensor(y[:, t, cols], acc, 1.5 * 0.0625, diff[t][:, cols], MULT, MULT)
+
+        def store_out(t, cols):
             nc.sync.dma_start(out_rows[:, t, cols], y[:, t, cols])
 
-        whole = slice(0, S)
         for t in range(PACK):
             nc.scalar.activation(
                 sg_win[t][:, :S],
@@ -242,24 +252,27 @@ def tile_picked_codesendgedb_none_po_kernel(
                 bias=bias[:, t : t + 1],
                 scale=sl_t[:, t : t + 1],
             )
-        for t in range(2):
+        for t in range(3):
             nc.vector.tensor_copy(far[t][:], sg_win[t][:].indirect(n4_t[:]))
-        nc.scalar.activation(far[2][:], sg_win[2][:].indirect(n4_t[:]), COPY)
+            subtract(nc.gpsimd, t, whole)
         for a in range(2):
             nc.scalar.activation(far[3][:, halves[a]], sg_win[3][:].indirect(n4_halves[a]), COPY)
-        subtract(0, whole)
-        subtract(1, whole)
-        scale_out(0, whole)
-        scale_out(1, whole)
-        subtract(2, whole)
-        subtract(3, halves[0])
-        scale_out(2, whole)
-        subtract(3, halves[1])
-        scale_out(3, halves[0])
-        scale_out(3, halves[1])
+        for a in range(2):
+            scale_out(0, halves[a], first2[a][:])
+        store_out(0, whole)
+        scale_out(1, whole, acc2[1][:])
+        store_out(1, whole)
+        subtract(nc.vector, 3, halves[0])
+        subtract(nc.vector, 3, halves[1])
+        for a in range(2):
+            scale_out(3, halves[a], acc2[3][:, halves[a]])
+        store_out(3, whole)
+        for a in range(2):
+            scale_out(2, halves[a], acc2[2][:, halves[a]])
+        store_out(2, whole)
         interleave(nc.scalar.copy, yb[0], y[:, :, halves[0]])
         interleave(nc.vector.tensor_copy, yb[1], y[:, :, halves[1]])
-        for a in (1, 0):
+        for a in range(2):
             nc.vector.quantize_mx(out=y_words[:, halves[a]].bitcast(FP8X4), scales=y_bytes[:, halves[a]], in_=yb[a][:])
             nc.sync.dma_start(out_words[:, halves[a]], y_words[:, halves[a]].bitcast(I32))
         for q in range(4):

@@ -21,11 +21,14 @@ SIGMOID = mybir.ActivationFunctionType.Sigmoid
 
 P = 128
 PACK = 4
+SCALE_ROWS = 16
+QUADRANT = 32
 HALF = S // 2
-LCOLS = S // 16
-LHALF = LCOLS // 2
-H_SPARE = 16
-DS_WIDE = 704
+LIST_COLS = S // 16
+LINE = 4
+SIXTEENTH = 0.0625
+H_WINDOW = S + 16
+DS_WINDOW = 704
 
 
 def tile_picked_codesendgedb_none_po_kernel(
@@ -38,29 +41,36 @@ def tile_picked_codesendgedb_none_po_kernel(
         shared = ctx.enter_context(tc.tile_pool(name="shared", bufs=1))
         psum = ctx.enter_context(tc.psum_pool(name="psum", bufs=1))
 
+        halves = [slice(0, HALF), slice(HALF, S)]
+        list_halves = [slice(0, LIST_COLS // 2), slice(LIST_COLS // 2, LIST_COLS)]
+        whole = slice(0, S)
+
+        def sb(shape, dtype, name):
+            return keep.tile(shape, dtype, name=name, align_bytes=64)
+
+        def bank(width, name, number):
+            return psum.tile([P, width], F32, name=name, tag="bank%d" % number)
+
         def load_list(src, name):
-            tile = lists.tile([P, LCOLS], U16, name=name)
+            tile = lists.tile([P, LIST_COLS], U16, name=name)
             nc.sync.dma_start(tile[:], src)
             return tile
 
-        def sb(shape, dtype, name, tag=None):
-            return keep.tile(shape, dtype, name=name, tag=tag or name, align_bytes=64)
-
         def words_view(dram):
             return dram[0].rearrange("p n t -> p (n t)").bitcast(I32)
+
+        def scale_rows_view(dram, width):
+            return dram[0].bitcast(I32).unsqueeze(1).to_broadcast([SCALE_ROWS, P // SCALE_ROWS, width // 4])
 
         d_byte_win = sb([P, G], U8, "d_byte_win")
         x_byte_win = sb([P, T], U8, "x_byte_win")
         d_word_win = sb([P, G], U32, "d_word_win")
         x_word_win = shared.tile([P, T], U32, name="x_word_win", offset=0, align_bytes=64)
 
-        def rows_view(dram, width):
-            return dram[0].bitcast(I32).unsqueeze(1).to_broadcast([16, 8, width // 4])
-
         offs_t = load_list(offs, "offs_t")
-        nc.sync.dma_start(x_byte_win[:].bitcast(I32), rows_view(x_scales, T))
+        nc.sync.dma_start(x_byte_win[:].bitcast(I32), scale_rows_view(x_scales, T))
         k1_t = load_list(k1, "k1_t")
-        nc.sync.dma_start(d_byte_win[:].bitcast(I32), rows_view(d_scales, G))
+        nc.sync.dma_start(d_byte_win[:].bitcast(I32), scale_rows_view(d_scales, G))
         nc.sync.dma_start(d_word_win[:].bitcast(I32), words_view(d_words))
         n2_t = load_list(n2, "n2_t")
         n1_t = load_list(n1, "n1_t")
@@ -73,7 +83,7 @@ def tile_picked_codesendgedb_none_po_kernel(
         w2_bytes = sb([P, H], U8, "w2_bytes")
         nc.vector.memset(placed1[:].bitcast(I32), 0)
         nc.vector.memset(w2_bytes[:].bitcast(I32), 0)
-        h_win = [sb([P, S + H_SPARE], F32, "h_win%d" % t) for t in range(PACK)]
+        h_win = [sb([P, H_WINDOW], F32, "h_win%d" % t) for t in range(PACK)]
         for t in range(PACK):
             nc.vector.memset(h_win[t][:, S:], 0.0)
 
@@ -91,63 +101,63 @@ def tile_picked_codesendgedb_none_po_kernel(
                 dealt.rearrange("p (t m) -> p t m", t=PACK), picked.rearrange("p (m t) -> p t m", t=PACK)
             )
 
-        def place_bytes(placed, dealt, queues):
-            for r in range(4):
-                queues[r % len(queues)].dma_start(placed[r:P:32, :].bitcast(I32), dealt[8 * r : P : 32, :].bitcast(I32))
-
         def deal_words(dealt, picked):
             nc.vector.tensor_copy(
-                dealt[:].rearrange("p (t m i) -> p m t i", t=PACK, i=4),
-                picked[:].rearrange("p (m i t) -> p m t i", t=PACK, i=4),
+                dealt[:].rearrange("p (t m i) -> p m t i", t=PACK, i=LINE),
+                picked[:].rearrange("p (m i t) -> p m t i", t=PACK, i=LINE),
             )
 
-        halves = [slice(0, HALF), slice(HALF, S)]
-        whole = slice(0, S)
-        w1_picked = sb([P, H], U8, "w1_picked")
-        xq_picked = sb([P, S], U8, "xq_picked")
+        def place_bytes(placed, dealt):
+            for r in range(4):
+                nc.sync.dma_start(
+                    placed[r:P:QUADRANT, :].bitcast(I32), dealt[8 * r : P : QUADRANT, :].bitcast(I32)
+                )
+
+        def product(out, w_words, w_bytes, t, moving_words, moving_bytes):
+            cols = slice(P * t, P * (t + 1))
+            nc.tensor.matmul_mx(
+                out=out,
+                lhsT=w_words[:, cols].bitcast(FP8X4),
+                lhsT_scale=w_bytes[:, cols],
+                rhs=moving_words.bitcast(FP8X4),
+                rhs_scale=moving_bytes,
+                start=True,
+                stop=True,
+            )
+
+        w1_bytes_picked = sb([P, H], U8, "w1_bytes_picked")
+        xq_bytes_picked = sb([P, S], U8, "xq_bytes_picked")
         dealt1 = sb([P, H + S], U8, "dealt1")
-        nc.vector.tensor_copy(xq_picked[:], x_byte_win[:].indirect(offs_t[:]))
-        nc.vector.tensor_copy(w1_picked[:], d_byte_win[:].indirect(k1_t[:]))
-        nc.vector.tensor_copy(dealt1[:, H:].bitcast(I32), xq_picked[:].bitcast(I32))
-        deal_bytes(dealt1[:, :H], w1_picked[:])
-        place_bytes(placed1, dealt1, [nc.sync])
+        nc.vector.tensor_copy(xq_bytes_picked[:], x_byte_win[:].indirect(offs_t[:]))
+        nc.vector.tensor_copy(w1_bytes_picked[:], d_byte_win[:].indirect(k1_t[:]))
+        nc.vector.tensor_copy(dealt1[:, H:].bitcast(I32), xq_bytes_picked[:].bitcast(I32))
+        deal_bytes(dealt1[:, :H], w1_bytes_picked[:])
+        place_bytes(placed1, dealt1)
         w1_bytes = placed1[:, :H]
         xq_bytes = placed1[:, H:]
         w1_words_picked = sb([P, H], U32, "w1_words_picked")
         w1_words = sb([P, H], U32, "w1_words")
         xq_words = sb([P, S], U32, "xq_words")
         nc.vector.tensor_copy(w1_words_picked[:], d_word_win[:].indirect(k1_t[:]))
-        nc.vector.tensor_copy(xq_words[:, halves[0]], x_word_win[:].indirect(offs_t[:, :LHALF]))
+        nc.vector.tensor_copy(xq_words[:, halves[0]], x_word_win[:].indirect(offs_t[:, list_halves[0]]))
         deal_words(w1_words, w1_words_picked)
-        nc.vector.tensor_copy(xq_words[:, halves[1]], x_word_win[:].indirect(offs_t[:, LHALF:]))
+        nc.vector.tensor_copy(xq_words[:, halves[1]], x_word_win[:].indirect(offs_t[:, list_halves[1]]))
 
-        def product(out, w_words, w_bytes, t, r_words, r_bytes):
-            cols = slice(P * t, P * (t + 1))
-            nc.tensor.matmul_mx(
-                out=out,
-                lhsT=w_words[:, cols].bitcast(FP8X4),
-                lhsT_scale=w_bytes[:, cols],
-                rhs=r_words.bitcast(FP8X4),
-                rhs_scale=r_bytes,
-                start=True,
-                stop=True,
-            )
-
-        first1 = [psum.tile([P, HALF], F32, name="first1_%d" % a, tag="bank%d" % a) for a in range(2)]
-        acc1 = [None] + [psum.tile([P, S], F32, name="acc1_%d" % t, tag="bank%d" % (t + 1)) for t in range(1, PACK)]
+        first1 = [bank(HALF, "first1_%d" % a, a) for a in range(2)]
+        acc1 = {t: bank(S, "acc1_%d" % t, t + 1) for t in range(1, PACK)}
         for a in range(2):
             product(first1[a][:], w1_words, w1_bytes, 0, xq_words[:, halves[a]], xq_bytes[:, halves[a]])
         for t in range(1, PACK):
             product(acc1[t][:], w1_words, w1_bytes, t, xq_words[:], xq_bytes)
 
-        w2_picked = shared.tile([P, H], U8, name="w2_picked", offset=4 * H, align_bytes=64)
+        w2_bytes_picked = shared.tile([P, H], U8, name="w2_bytes_picked", offset=4 * H, align_bytes=64)
         w2_words_picked = shared.tile([P, H], U32, name="w2_words_picked", offset=0, align_bytes=64)
         dealt2 = sb([P, H], U8, "dealt2")
         w2_words = sb([P, H], U32, "w2_words")
-        nc.vector.tensor_copy(w2_picked[:], d_byte_win[:].indirect(k2_t[:]))
+        nc.vector.tensor_copy(w2_bytes_picked[:], d_byte_win[:].indirect(k2_t[:]))
         nc.vector.tensor_copy(w2_words_picked[:], d_word_win[:].indirect(k2_t[:]))
-        deal_bytes(dealt2[:], w2_picked[:])
-        place_bytes(w2_bytes, dealt2, [nc.sync])
+        deal_bytes(dealt2[:], w2_bytes_picked[:])
+        place_bytes(w2_bytes, dealt2)
         deal_words(w2_words, w2_words_picked)
         bias = sb([P, PACK], F32, "bias")
         sl_th = sb([P, PACK], F32, "sl_th")
@@ -156,127 +166,111 @@ def tile_picked_codesendgedb_none_po_kernel(
 
         h2_win = [sb([P, 2 * S], F32, "h2_win%d" % t) for t in range(PACK)]
         sg_win = [sb([P, 2 * S], F32, "sg_win%d" % t) for t in range(PACK)]
-        fetched = [sg_win[t][:, S:] for t in range(PACK)]
+        sig_h = [h2_win[t][:, S:] for t in range(PACK)]
+        h_n2 = [sg_win[t][:, S:] for t in range(PACK)]
         sm = [sb([P, S], F32, "sm%d" % t) for t in range(PACK)]
-        ds = [sb([P, DS_WIDE if t in (0, 3) else S], F32, "ds%d" % t) for t in range(PACK)]
+        vector_tiles = (0, 3)
+        ds = [sb([P, DS_WINDOW if t in vector_tiles else S], F32, "ds%d" % t) for t in range(PACK)]
         z = sb([P, PACK, S], F32, "z")
 
-        for t in range(PACK):
-            if t == 0:
-                nc.scalar.activation(h2_win[0][:, S : S + HALF], first1[0][:], SIGMOID, scale=0.0625)
-                for a in range(2):
-                    nc.scalar.activation(h_win[0][:, halves[a]], first1[a][:], COPY, scale=0.0625)
-                nc.scalar.activation(h2_win[0][:, S + HALF :], first1[1][:], SIGMOID, scale=0.0625)
-            else:
-                nc.scalar.activation(h_win[t][:, :S], acc1[t][:], COPY, scale=0.0625)
-            nc.scalar.activation(fetched[t], h_win[t][:].indirect(n2_t[:]), COPY)
-            if t == 0:
-                nc.vector.tensor_tensor(sm[t][:], h_win[t][:, :S], fetched[t], MAX)
-            else:
-                nc.vector.scalar_tensor_tensor(sm[t][:], acc1[t][:], 0.0625, fetched[t], MULT, MAX)
-            if t in (0, 3):
+        nc.scalar.activation(sig_h[0][:, halves[0]], first1[0][:], SIGMOID, scale=SIXTEENTH)
+        for a in range(2):
+            nc.scalar.activation(h_win[0][:, halves[a]], first1[a][:], COPY, scale=SIXTEENTH)
+        nc.scalar.activation(sig_h[0][:, halves[1]], first1[1][:], SIGMOID, scale=SIXTEENTH)
+        nc.scalar.activation(h_n2[0], h_win[0][:].indirect(n2_t[:]), COPY)
+        nc.vector.tensor_tensor(sm[0][:], h_win[0][:, whole], h_n2[0], MAX)
+        nc.vector.tensor_copy(ds[0][:].indirect(n1_t[:]), sm[0][:])
+        for t in range(1, PACK):
+            nc.scalar.activation(h_win[t][:, whole], acc1[t][:], COPY, scale=SIXTEENTH)
+            nc.scalar.activation(h_n2[t], h_win[t][:].indirect(n2_t[:]), COPY)
+            nc.vector.scalar_tensor_tensor(sm[t][:], acc1[t][:], SIXTEENTH, h_n2[t], MULT, MAX)
+            if t in vector_tiles:
                 nc.vector.tensor_copy(ds[t][:].indirect(n1_t[:]), sm[t][:])
             if t == 1:
-                nc.vector.tensor_copy(ds[1][:].indirect(n1_t[:, :14]), sm[1][:, :224])
+                nc.vector.tensor_copy(ds[1][:].indirect(n1_t[:, list_halves[0]]), sm[1][:, halves[0]])
         for t in range(1, PACK):
-            nc.scalar.activation(h2_win[t][:, S:], h_win[t][:, :S], SIGMOID)
-
-        nc.scalar.activation(ds[1][:].indirect(n1_t[:, 14:]), sm[1][:, 224:], COPY)
-        nc.scalar.activation(ds[2][:].indirect(n1_t[:, :LHALF]), sm[2][:, :HALF], COPY)
-        nc.scalar.activation(ds[2][:].indirect(n1_t[:, LHALF:]), sm[2][:, HALF:], COPY)
+            nc.scalar.activation(sig_h[t], h_win[t][:, whole], SIGMOID)
+        for t, a in ((1, 1), (2, 0), (2, 1)):
+            nc.scalar.activation(ds[t][:].indirect(n1_t[:, list_halves[a]]), sm[t][:, halves[a]], COPY)
 
         gated = [sb([P, S], F32, "gated%d" % t) for t in range(2)]
         for t in range(2):
-            nc.gpsimd.tensor_scalar(gated[t][:], h2_win[t][:, S:], gs_t[:, t : t + 1], 0.0, MULT, ADD)
-            nc.gpsimd.tensor_tensor(z[:, t, :], ds[t][:, :S], gated[t][:], MULT)
-        nc.vector.scalar_tensor_tensor(z[:, 3, :], ds[3][:, :S], gs_t[:, 3:4], h2_win[3][:, S:], MULT, MULT)
-        for a in range(2):
-            nc.vector.scalar_tensor_tensor(
-                z[:, 2, halves[a]],
-                ds[2][:, halves[a]],
-                gs_t[:, 2:3],
-                h2_win[2][:, S + HALF * a : S + HALF * (a + 1)],
-                MULT,
-                MULT,
+            nc.gpsimd.tensor_scalar(gated[t][:], sig_h[t], gs_t[:, t : t + 1], 0.0, MULT, ADD)
+            nc.gpsimd.tensor_tensor(z[:, t, :], ds[t][:, whole], gated[t][:], MULT)
+        for t, cols in ((3, whole), (2, halves[0]), (2, halves[1])):
+            nc.vector.scalar_tensor_tensor(z[:, t, cols], ds[t][:, cols], gs_t[:, t : t + 1], sig_h[t][:, cols], MULT, MULT)
+
+        def interleave(copy, dst, src):
+            copy(
+                dst[:].rearrange("p (c i t) -> p c t i", i=LINE, t=PACK),
+                src.rearrange("p t (c i) -> p c t i", i=LINE),
             )
 
-        def interleave(eng_copy, dst, src):
-            eng_copy(
-                dst[:].rearrange("p (c i t) -> p c t i", i=4, t=PACK),
-                src.rearrange("p t (c i) -> p c t i", i=4),
-            )
-
-        zb = [sb([P, PACK * HALF], BF16, "zb%d" % a) for a in range(2)]
+        z_bf16 = [sb([P, PACK * HALF], BF16, "z_bf16_%d" % a) for a in range(2)]
         z_words = sb([P, S], U32, "z_words")
         z_bytes = sb([P, S], U8, "z_bytes")
         for a in range(2):
-            interleave(nc.vector.tensor_copy, zb[a], z[:, :, halves[a]])
+            interleave(nc.vector.tensor_copy, z_bf16[a], z[:, :, halves[a]])
         for a in range(2):
-            nc.vector.quantize_mx(out=z_words[:, halves[a]].bitcast(FP8X4), scales=z_bytes[:, halves[a]], in_=zb[a][:])
+            nc.vector.quantize_mx(
+                out=z_words[:, halves[a]].bitcast(FP8X4), scales=z_bytes[:, halves[a]], in_=z_bf16[a][:]
+            )
 
-        first2 = [psum.tile([P, HALF], F32, name="first2_%d" % a, tag="bank%d" % (5 + a)) for a in range(2)]
-        acc2 = [None] + [psum.tile([P, S], F32, name="acc2_%d" % t, tag="bank%d" % ((6 + t) % 8)) for t in range(1, PACK)]
+        first2 = [bank(HALF, "first2_%d" % a, 5 + a) for a in range(2)]
+        acc2 = {t: bank(S, "acc2_%d" % t, (6 + t) % 8) for t in range(1, PACK)}
         for a in range(2):
             product(first2[a][:], w2_words, w2_bytes, 0, z_words[:, halves[a]], z_bytes[:, halves[a]])
         for t in range(1, PACK):
             product(acc2[t][:], w2_words, w2_bytes, t, z_words[:], z_bytes[:])
         for a in range(2):
-            nc.scalar.activation(h2_win[0][:, halves[a]], first2[a][:], COPY, scale=0.0625)
+            nc.scalar.activation(h2_win[0][:, halves[a]], first2[a][:], COPY, scale=SIXTEENTH)
         for t in range(1, PACK):
-            nc.vector.tensor_scalar(h2_win[t][:, :S], acc2[t][:], 0.0625, None, MULT)
+            nc.vector.tensor_scalar(h2_win[t][:, whole], acc2[t][:], SIXTEENTH, None, MULT)
 
-        far = [sb([P, S], F32, "far%d" % t) for t in range(PACK)]
+        sg_n4 = [sb([P, S], F32, "sg_n4_%d" % t) for t in range(PACK)]
         diff = [sb([P, S], F32, "diff%d" % t) for t in range(PACK)]
         y = sb([P, PACK, S], F32, "y")
-        yb = [sb([P, PACK * HALF], BF16, "yb%d" % a) for a in range(2)]
+        y_bf16 = [sb([P, PACK * HALF], BF16, "y_bf16_%d" % a) for a in range(2)]
         y_words = sb([P, S], U32, "y_words")
         y_bytes = sb([P, S], U8, "y_bytes")
-        n4_halves = [n4_t[:, :LHALF], n4_t[:, LHALF:]]
         out_rows = out_0.rearrange("(p t) c -> p t c", t=PACK)
-        out_words = out_1[0].rearrange("p n t -> p (n t)").bitcast(I32)
+        out_words = words_view(out_1)
 
-        def subtract(engine, t, cols):
-            engine.tensor_tensor(diff[t][:, cols], sg_win[t][:, cols], far[t][:, cols], SUB)
+        def subtract(t, cols):
+            nc.vector.tensor_tensor(diff[t][:, cols], sg_win[t][:, cols], sg_n4[t][:, cols], SUB)
 
-        def scale_out(t, cols, acc):
-            nc.vector.scalar_tensor_tensor(y[:, t, cols], acc, 1.5 * 0.0625, diff[t][:, cols], MULT, MULT)
-
-        def store_out(t, cols):
+        def finish(t, cols):
+            nc.vector.scalar_tensor_tensor(y[:, t, cols], h2_win[t][:, cols], 1.5, diff[t][:, cols], MULT, MULT)
             nc.sync.dma_start(out_rows[:, t, cols], y[:, t, cols])
 
         for t in range(PACK):
             nc.scalar.activation(
-                sg_win[t][:, :S],
+                sg_win[t][:, whole],
                 h2_win[t][:].indirect(n3_t[:]),
                 SIGMOID,
                 bias=bias[:, t : t + 1],
                 scale=sl_t[:, t : t + 1],
             )
-        for t in range(3):
-            nc.vector.tensor_copy(far[t][:], sg_win[t][:].indirect(n4_t[:]))
-            subtract(nc.gpsimd, t, whole)
+        for t in range(2):
+            nc.vector.tensor_copy(sg_n4[t][:], sg_win[t][:].indirect(n4_t[:]))
+        nc.scalar.activation(sg_n4[2][:], sg_win[2][:].indirect(n4_t[:]), COPY)
         for a in range(2):
-            nc.scalar.activation(far[3][:, halves[a]], sg_win[3][:].indirect(n4_halves[a]), COPY)
+            nc.scalar.activation(sg_n4[3][:, halves[a]], sg_win[3][:].indirect(n4_t[:, list_halves[a]]), COPY)
+        for pair in (((0, whole), (1, whole)), ((2, whole), (3, halves[0])), ((3, halves[1]),)):
+            for t, cols in pair:
+                subtract(t, cols)
+            for t, cols in pair:
+                finish(t, cols)
+        interleave(nc.scalar.copy, y_bf16[0], y[:, :, halves[0]])
+        interleave(nc.vector.tensor_copy, y_bf16[1], y[:, :, halves[1]])
         for a in range(2):
-            scale_out(0, halves[a], first2[a][:])
-        store_out(0, whole)
-        scale_out(1, whole, acc2[1][:])
-        store_out(1, whole)
-        subtract(nc.vector, 3, halves[0])
-        subtract(nc.vector, 3, halves[1])
-        for a in range(2):
-            scale_out(3, halves[a], acc2[3][:, halves[a]])
-        store_out(3, whole)
-        for a in range(2):
-            scale_out(2, halves[a], acc2[2][:, halves[a]])
-        store_out(2, whole)
-        interleave(nc.scalar.copy, yb[0], y[:, :, halves[0]])
-        interleave(nc.vector.tensor_copy, yb[1], y[:, :, halves[1]])
-        for a in range(2):
-            nc.vector.quantize_mx(out=y_words[:, halves[a]].bitcast(FP8X4), scales=y_bytes[:, halves[a]], in_=yb[a][:])
+            nc.vector.quantize_mx(
+                out=y_words[:, halves[a]].bitcast(FP8X4), scales=y_bytes[:, halves[a]], in_=y_bf16[a][:]
+            )
             nc.sync.dma_start(out_words[:, halves[a]], y_words[:, halves[a]].bitcast(I32))
         for q in range(4):
             queue = nc.scalar if q % 2 == 0 else nc.sync
             queue.dma_start(
-                out_2[0, 4 * q : 4 * q + 4, :].bitcast(I32), y_bytes[32 * q : 32 * q + 4, :].bitcast(I32)
+                out_2[0, 4 * q : 4 * q + 4, :].bitcast(I32),
+                y_bytes[QUADRANT * q : QUADRANT * q + 4, :].bitcast(I32),
             )

from contextlib import ExitStack

import concourse.mybir as mybir

K, T, S, G, H = 512, 1024, 512, 2048, 512
FLOPS = 2 * 2 * K * H * S

F32 = mybir.dt.float32
BF16 = mybir.dt.bfloat16
I32 = mybir.dt.int32
U32 = mybir.dt.uint32
U16 = mybir.dt.uint16
U8 = mybir.dt.uint8
FP8X4 = mybir.dt.float8_e4m3fn_x4
MULT = mybir.AluOpType.mult
MAX = mybir.AluOpType.max
ADD = mybir.AluOpType.add
SUB = mybir.AluOpType.subtract
COPY = mybir.ActivationFunctionType.Copy
SIGMOID = mybir.ActivationFunctionType.Sigmoid

P = 128
PACK = 4
SCALE_ROWS = 16
QUADRANT = 32
HALF = S // 2
LIST_COLS = S // 16
LINE = 4
SIXTEENTH = 0.0625
H_WINDOW = S + 16
DS_WINDOW = 704


def tile_picked_codesendgedb_none_po_kernel(
    tc, x_words, x_scales, d_words, d_scales, gs, sl, th, offs, k1, n1, n2, k2, n3, n4, out_0, out_1, out_2
):
    nc = tc.nc
    with ExitStack() as ctx:
        lists = ctx.enter_context(tc.tile_pool(name="lists", bufs=1))
        keep = ctx.enter_context(tc.tile_pool(name="keep", bufs=1))
        shared = ctx.enter_context(tc.tile_pool(name="shared", bufs=1))
        psum = ctx.enter_context(tc.psum_pool(name="psum", bufs=1))

        halves = [slice(0, HALF), slice(HALF, S)]
        list_halves = [slice(0, LIST_COLS // 2), slice(LIST_COLS // 2, LIST_COLS)]
        whole = slice(0, S)

        def sb(shape, dtype, name):
            return keep.tile(shape, dtype, name=name, align_bytes=64)

        def bank(width, name, number):
            return psum.tile([P, width], F32, name=name, tag="bank%d" % number)

        def load_list(src, name):
            tile = lists.tile([P, LIST_COLS], U16, name=name)
            nc.sync.dma_start(tile[:], src)
            return tile

        def words_view(dram):
            return dram[0].rearrange("p n t -> p (n t)").bitcast(I32)

        def scale_rows_view(dram, width):
            return dram[0].bitcast(I32).unsqueeze(1).to_broadcast([SCALE_ROWS, P // SCALE_ROWS, width // 4])

        d_byte_win = sb([P, G], U8, "d_byte_win")
        x_byte_win = sb([P, T], U8, "x_byte_win")
        d_word_win = sb([P, G], U32, "d_word_win")
        x_word_win = shared.tile([P, T], U32, name="x_word_win", offset=0, align_bytes=64)

        offs_t = load_list(offs, "offs_t")
        nc.sync.dma_start(x_byte_win[:].bitcast(I32), scale_rows_view(x_scales, T))
        k1_t = load_list(k1, "k1_t")
        nc.sync.dma_start(d_byte_win[:].bitcast(I32), scale_rows_view(d_scales, G))
        nc.sync.dma_start(d_word_win[:].bitcast(I32), words_view(d_words))
        n2_t = load_list(n2, "n2_t")
        n1_t = load_list(n1, "n1_t")
        n3_t = load_list(n3, "n3_t")
        nc.sync.dma_start(x_word_win[:].bitcast(I32), words_view(x_words))
        n4_t = load_list(n4, "n4_t")
        k2_t = load_list(k2, "k2_t")

        placed1 = sb([P, H + S], U8, "placed1")
        w2_bytes = sb([P, H], U8, "w2_bytes")
        nc.vector.memset(placed1[:].bitcast(I32), 0)
        nc.vector.memset(w2_bytes[:].bitcast(I32), 0)
        h_win = [sb([P, H_WINDOW], F32, "h_win%d" % t) for t in range(PACK)]
        for t in range(PACK):
            nc.vector.memset(h_win[t][:, S:], 0.0)

        def load_rows(src, name):
            tile = sb([P, PACK], F32, name)
            nc.gpsimd.dma_start(tile[:], src.rearrange("(p t) o -> p (t o)", t=PACK))
            return tile

        gs_t = load_rows(gs, "gs_t")
        sl_t = load_rows(sl, "sl_t")
        th_t = load_rows(th, "th_t")

        def deal_bytes(dealt, picked):
            nc.vector.tensor_copy(
                dealt.rearrange("p (t m) -> p t m", t=PACK), picked.rearrange("p (m t) -> p t m", t=PACK)
            )

        def deal_words(dealt, picked):
            nc.vector.tensor_copy(
                dealt[:].rearrange("p (t m i) -> p m t i", t=PACK, i=LINE),
                picked[:].rearrange("p (m i t) -> p m t i", t=PACK, i=LINE),
            )

        def place_bytes(placed, dealt):
            for r in range(4):
                nc.sync.dma_start(
                    placed[r:P:QUADRANT, :].bitcast(I32), dealt[8 * r : P : QUADRANT, :].bitcast(I32)
                )

        def product(out, w_words, w_bytes, t, moving_words, moving_bytes):
            cols = slice(P * t, P * (t + 1))
            nc.tensor.matmul_mx(
                out=out,
                lhsT=w_words[:, cols].bitcast(FP8X4),
                lhsT_scale=w_bytes[:, cols],
                rhs=moving_words.bitcast(FP8X4),
                rhs_scale=moving_bytes,
                start=True,
                stop=True,
            )

        w1_bytes_picked = sb([P, H], U8, "w1_bytes_picked")
        xq_bytes_picked = sb([P, S], U8, "xq_bytes_picked")
        dealt1 = sb([P, H + S], U8, "dealt1")
        nc.vector.tensor_copy(xq_bytes_picked[:], x_byte_win[:].indirect(offs_t[:]))
        nc.vector.tensor_copy(w1_bytes_picked[:], d_byte_win[:].indirect(k1_t[:]))
        nc.vector.tensor_copy(dealt1[:, H:].bitcast(I32), xq_bytes_picked[:].bitcast(I32))
        deal_bytes(dealt1[:, :H], w1_bytes_picked[:])
        place_bytes(placed1, dealt1)
        w1_bytes = placed1[:, :H]
        xq_bytes = placed1[:, H:]
        w1_words_picked = sb([P, H], U32, "w1_words_picked")
        w1_words = sb([P, H], U32, "w1_words")
        xq_words = sb([P, S], U32, "xq_words")
        nc.vector.tensor_copy(w1_words_picked[:], d_word_win[:].indirect(k1_t[:]))
        nc.vector.tensor_copy(xq_words[:, halves[0]], x_word_win[:].indirect(offs_t[:, list_halves[0]]))
        deal_words(w1_words, w1_words_picked)
        nc.vector.tensor_copy(xq_words[:, halves[1]], x_word_win[:].indirect(offs_t[:, list_halves[1]]))

        first1 = [bank(HALF, "first1_%d" % a, a) for a in range(2)]
        acc1 = {t: bank(S, "acc1_%d" % t, t + 1) for t in range(1, PACK)}
        for a in range(2):
            product(first1[a][:], w1_words, w1_bytes, 0, xq_words[:, halves[a]], xq_bytes[:, halves[a]])
        for t in range(1, PACK):
            product(acc1[t][:], w1_words, w1_bytes, t, xq_words[:], xq_bytes)

        w2_bytes_picked = shared.tile([P, H], U8, name="w2_bytes_picked", offset=4 * H, align_bytes=64)
        w2_words_picked = shared.tile([P, H], U32, name="w2_words_picked", offset=0, align_bytes=64)
        dealt2 = sb([P, H], U8, "dealt2")
        w2_words = sb([P, H], U32, "w2_words")
        nc.vector.tensor_copy(w2_bytes_picked[:], d_byte_win[:].indirect(k2_t[:]))
        nc.vector.tensor_copy(w2_words_picked[:], d_word_win[:].indirect(k2_t[:]))
        deal_bytes(dealt2[:], w2_bytes_picked[:])
        place_bytes(w2_bytes, dealt2)
        deal_words(w2_words, w2_words_picked)
        bias = sb([P, PACK], F32, "bias")
        sl_th = sb([P, PACK], F32, "sl_th")
        nc.gpsimd.tensor_tensor(sl_th[:], sl_t[:], th_t[:], MULT)
        nc.gpsimd.tensor_scalar(bias[:], sl_th[:], -1.0, 0.0, MULT, ADD)

        h2_win = [sb([P, 2 * S], F32, "h2_win%d" % t) for t in range(PACK)]
        sg_win = [sb([P, 2 * S], F32, "sg_win%d" % t) for t in range(PACK)]
        sig_h = [h2_win[t][:, S:] for t in range(PACK)]
        h_n2 = [sg_win[t][:, S:] for t in range(PACK)]
        sm = [sb([P, S], F32, "sm%d" % t) for t in range(PACK)]
        vector_tiles = (0, 3)
        ds = [sb([P, DS_WINDOW if t in vector_tiles else S], F32, "ds%d" % t) for t in range(PACK)]
        z = sb([P, PACK, S], F32, "z")

        nc.scalar.activation(sig_h[0][:, halves[0]], first1[0][:], SIGMOID, scale=SIXTEENTH)
        for a in range(2):
            nc.scalar.activation(h_win[0][:, halves[a]], first1[a][:], COPY, scale=SIXTEENTH)
        nc.scalar.activation(sig_h[0][:, halves[1]], first1[1][:], SIGMOID, scale=SIXTEENTH)
        nc.scalar.activation(h_n2[0], h_win[0][:].indirect(n2_t[:]), COPY)
        nc.vector.tensor_tensor(sm[0][:], h_win[0][:, whole], h_n2[0], MAX)
        nc.vector.tensor_copy(ds[0][:].indirect(n1_t[:]), sm[0][:])
        for t in range(1, PACK):
            nc.scalar.activation(h_win[t][:, whole], acc1[t][:], COPY, scale=SIXTEENTH)
            nc.scalar.activation(h_n2[t], h_win[t][:].indirect(n2_t[:]), COPY)
            nc.vector.scalar_tensor_tensor(sm[t][:], acc1[t][:], SIXTEENTH, h_n2[t], MULT, MAX)
            if t in vector_tiles:
                nc.vector.tensor_copy(ds[t][:].indirect(n1_t[:]), sm[t][:])
            if t == 1:
                nc.vector.tensor_copy(ds[1][:].indirect(n1_t[:, list_halves[0]]), sm[1][:, halves[0]])
        for t in range(1, PACK):
            nc.scalar.activation(sig_h[t], h_win[t][:, whole], SIGMOID)
        for t, a in ((1, 1), (2, 0), (2, 1)):
            nc.scalar.activation(ds[t][:].indirect(n1_t[:, list_halves[a]]), sm[t][:, halves[a]], COPY)

        gated = [sb([P, S], F32, "gated%d" % t) for t in range(2)]
        for t in range(2):
            nc.gpsimd.tensor_scalar(gated[t][:], sig_h[t], gs_t[:, t : t + 1], 0.0, MULT, ADD)
            nc.gpsimd.tensor_tensor(z[:, t, :], ds[t][:, whole], gated[t][:], MULT)
        for t, cols in ((3, whole), (2, halves[0]), (2, halves[1])):
            nc.vector.scalar_tensor_tensor(z[:, t, cols], ds[t][:, cols], gs_t[:, t : t + 1], sig_h[t][:, cols], MULT, MULT)

        def interleave(copy, dst, src):
            copy(
                dst[:].rearrange("p (c i t) -> p c t i", i=LINE, t=PACK),
                src.rearrange("p t (c i) -> p c t i", i=LINE),
            )

        z_bf16 = [sb([P, PACK * HALF], BF16, "z_bf16_%d" % a) for a in range(2)]
        z_words = sb([P, S], U32, "z_words")
        z_bytes = sb([P, S], U8, "z_bytes")
        for a in range(2):
            interleave(nc.vector.tensor_copy, z_bf16[a], z[:, :, halves[a]])
        for a in range(2):
            nc.vector.quantize_mx(
                out=z_words[:, halves[a]].bitcast(FP8X4), scales=z_bytes[:, halves[a]], in_=z_bf16[a][:]
            )

        first2 = [bank(HALF, "first2_%d" % a, 5 + a) for a in range(2)]
        acc2 = {t: bank(S, "acc2_%d" % t, (6 + t) % 8) for t in range(1, PACK)}
        for a in range(2):
            product(first2[a][:], w2_words, w2_bytes, 0, z_words[:, halves[a]], z_bytes[:, halves[a]])
        for t in range(1, PACK):
            product(acc2[t][:], w2_words, w2_bytes, t, z_words[:], z_bytes[:])
        for a in range(2):
            nc.scalar.activation(h2_win[0][:, halves[a]], first2[a][:], COPY, scale=SIXTEENTH)
        for t in range(1, PACK):
            nc.vector.tensor_scalar(h2_win[t][:, whole], acc2[t][:], SIXTEENTH, None, MULT)

        sg_n4 = [sb([P, S], F32, "sg_n4_%d" % t) for t in range(PACK)]
        diff = [sb([P, S], F32, "diff%d" % t) for t in range(PACK)]
        y = sb([P, PACK, S], F32, "y")
        y_bf16 = [sb([P, PACK * HALF], BF16, "y_bf16_%d" % a) for a in range(2)]
        y_words = sb([P, S], U32, "y_words")
        y_bytes = sb([P, S], U8, "y_bytes")
        out_rows = out_0.rearrange("(p t) c -> p t c", t=PACK)
        out_words = words_view(out_1)

        def subtract(t, cols):
            nc.vector.tensor_tensor(diff[t][:, cols], sg_win[t][:, cols], sg_n4[t][:, cols], SUB)

        def finish(t, cols):
            nc.vector.scalar_tensor_tensor(y[:, t, cols], h2_win[t][:, cols], 1.5, diff[t][:, cols], MULT, MULT)
            nc.sync.dma_start(out_rows[:, t, cols], y[:, t, cols])

        for t in range(PACK):
            nc.scalar.activation(
                sg_win[t][:, whole],
                h2_win[t][:].indirect(n3_t[:]),
                SIGMOID,
                bias=bias[:, t : t + 1],
                scale=sl_t[:, t : t + 1],
            )
        for t in range(2):
            nc.vector.tensor_copy(sg_n4[t][:], sg_win[t][:].indirect(n4_t[:]))
        nc.scalar.activation(sg_n4[2][:], sg_win[2][:].indirect(n4_t[:]), COPY)
        for a in range(2):
            nc.scalar.activation(sg_n4[3][:, halves[a]], sg_win[3][:].indirect(n4_t[:, list_halves[a]]), COPY)
        for pair in (((0, whole), (1, whole)), ((2, whole), (3, halves[0])), ((3, halves[1]),)):
            for t, cols in pair:
                subtract(t, cols)
            for t, cols in pair:
                finish(t, cols)
        interleave(nc.scalar.copy, y_bf16[0], y[:, :, halves[0]])
        interleave(nc.vector.tensor_copy, y_bf16[1], y[:, :, halves[1]])
        for a in range(2):
            nc.vector.quantize_mx(
                out=y_words[:, halves[a]].bitcast(FP8X4), scales=y_bytes[:, halves[a]], in_=y_bf16[a][:]
            )
            nc.sync.dma_start(out_words[:, halves[a]], y_words[:, halves[a]].bitcast(I32))
        for q in range(4):
            queue = nc.scalar if q % 2 == 0 else nc.sync
            queue.dma_start(
                out_2[0, 4 * q : 4 * q + 4, :].bitcast(I32),
                y_bytes[QUADRANT * q : QUADRANT * q + 4, :].bitcast(I32),
            )
